import numpy as np
import ml_dtypes

BF16 = ml_dtypes.bfloat16


def bf(x):
    return np.asarray(x, np.float32).astype(BF16)


def f32(x):
    return np.asarray(x, np.float32)


def f64(x):
    return np.asarray(x).astype(np.float64)


def striped(idx):
    return np.tile(idx.reshape(-1, 16).T, (8, 1))


S, K, N, V, D, H, O = 1024, 256, 512, 256, 2, 256, 256


def sigmoid(v):
    return 1.0 / (1.0 + np.exp(-v))


def setup_inputs():
    return {"table": bf(np.random.standard_normal((K, S))), "w": bf(np.random.standard_normal((D, K, H)) / np.sqrt(D * K)), "b": f32(0.5 * np.random.standard_normal((H, 1))), "w2": bf(np.random.standard_normal((H, O)) / np.sqrt(H)), "r": f32(np.random.standard_normal((O, V))), "offs": striped(np.random.permutation(np.tile(np.arange(S), 2))[:N])}


def reference(table, w, b, w2, r, offs):
    idx = offs[:16].T.reshape(-1)
    x = f64(table)[:, idx]
    t = sum(f64(w)[d].T @ x[:, d * V : (d + 1) * V] for d in range(D)) + f64(b)
    t = t * sigmoid(t)
    return f64(w2).T @ t + f64(r)

@@ -1,0 +1,68 @@
+import concourse.mybir as mybir
+
+S, K, V, D, H, O = 1024, 256, 256, 2, 256, 256
+N = D * V
+P = 128
+GROUP = 16
+KB, HB, OB = K // P, H // P, O // P
+
+FLOPS = 2 * D * K * H * V + 2 * H * O * V
+
+BF16, F32, U16 = mybir.dt.bfloat16, mybir.dt.float32, mybir.dt.uint16
+SILU = mybir.ActivationFunctionType.Silu
+ADD = mybir.AluOpType.add
+
+
+def tile_rows_edge2_silu_rep_kernel(tc, table, w, b, w2, r, offs, out):
+    nc = tc.nc
+    with (
+        tc.tile_pool(name="sbuf", bufs=1) as sbuf,
+        tc.psum_pool(name="psum", bufs=1) as psum,
+    ):
+        table_blocks = table.rearrange("(p a) s -> a p s", a=KB)
+        w_ends = w.rearrange("d (p a) i -> d p (a i)", a=KB)
+
+        nodes = [sbuf.tile([P, S], BF16, name=f"nodes{a}") for a in range(KB)]
+        w1 = [sbuf.tile([P, KB * H], BF16, name=f"w1_{d}") for d in range(D)]
+        offsets = sbuf.tile([P, N // GROUP], U16)
+        bias = sbuf.tile([P, HB], F32)
+        w2_t = sbuf.tile([P, HB, O], BF16)
+        r_t = sbuf.tile([P, OB, V], F32)
+
+        nc.sync.dma_start(nodes[0][:], table_blocks[0])
+        nc.sync.dma_start(w1[0][:], w_ends[0])
+        nc.sync.dma_start(offsets[:], offs)
+        nc.sync.dma_start(w1[1][:], w_ends[1])
+        nc.sync.dma_start(nodes[1][:], table_blocks[1])
+        nc.sync.dma_start(w2_t[:], w2.rearrange("(c p) o -> p c o", p=P))
+        nc.sync.dma_start(r_t[:], r.rearrange("(e p) v -> p e v", p=P))
+        nc.scalar.dma_start(bias[:], b.rearrange("(c p) o -> p (c o)", p=P))
+
+        pre = [psum.tile([P, V], F32, name=f"pre{c}") for c in range(HB)]
+        cols = V // GROUP
+        for a in range(KB):
+            last = a == KB - 1
+            order = [(d, c) for c in range(HB) for d in range(D)] if last else [(d, c) for d in range(D) for c in range(HB)]
+            for d, c in order:
+                nc.tensor.matmul(
+                    pre[c][:],
+                    w1[d][:, a * H + c * P : a * H + (c + 1) * P],
+                    nodes[a][:].indirect(offsets[:, d * cols : (d + 1) * cols]),
+                    start=(a == 0 and d == 0),
+                    stop=(last and d == D - 1),
+                )
+        h = [sbuf.tile([P, V], BF16, name=f"h{c}") for c in range(HB)]
+        for c in range(HB):
+            nc.scalar.activation(h[c][:], pre[c][:], SILU, bias=bias[:, c : c + 1])
+
+        update = [psum.tile([P, V], F32, name=f"update{e}") for e in range(OB)]
+        for c in range(HB):
+            for e in range(OB):
+                nc.tensor.matmul(
+                    update[e][:], w2_t[:, c, e * P : (e + 1) * P], h[c][:],
+                    start=(c == 0), stop=(c == HB - 1),
+                )
+        for e in range(OB):
+            result = sbuf.tile([P, V], F32, name=f"result{e}")
+            nc.vector.tensor_tensor(result[:], update[e][:], r_t[:, e, :], ADD)
+            nc.sync.dma_start(out[e * P : (e + 1) * P, :], result[:])

@@ -5,6 +5,7 @@ N = D * V
 P = 128
 GROUP = 16
 KB, HB, OB = K // P, H // P, O // P
+HALF = V // 2
 
 FLOPS = 2 * D * K * H * V + 2 * H * O * V
 
@@ -32,37 +33,50 @@ def tile_rows_edge2_silu_rep_kernel(tc, table, w, b, w2, r, offs, out):
         nc.sync.dma_start(nodes[0][:], table_blocks[0])
         nc.sync.dma_start(w1[0][:], w_ends[0])
         nc.sync.dma_start(offsets[:], offs)
+        nc.sync.dma_start(bias[:], b.rearrange("(c p) o -> p (c o)", p=P))
         nc.sync.dma_start(w1[1][:], w_ends[1])
         nc.sync.dma_start(nodes[1][:], table_blocks[1])
         nc.sync.dma_start(w2_t[:], w2.rearrange("(c p) o -> p c o", p=P))
         nc.sync.dma_start(r_t[:], r.rearrange("(e p) v -> p e v", p=P))
-        nc.scalar.dma_start(bias[:], b.rearrange("(c p) o -> p (c o)", p=P))
 
-        pre = [psum.tile([P, V], F32, name=f"pre{c}") for c in range(HB)]
-        cols = V // GROUP
-        for a in range(KB):
-            last = a == KB - 1
-            order = [(d, c) for c in range(HB) for d in range(D)] if last else [(d, c) for d in range(D) for c in range(HB)]
-            for d, c in order:
-                nc.tensor.matmul(
-                    pre[c][:],
-                    w1[d][:, a * H + c * P : a * H + (c + 1) * P],
-                    nodes[a][:].indirect(offsets[:, d * cols : (d + 1) * cols]),
-                    start=(a == 0 and d == 0),
-                    stop=(last and d == D - 1),
-                )
-        h = [sbuf.tile([P, V], BF16, name=f"h{c}") for c in range(HB)]
-        for c in range(HB):
-            nc.scalar.activation(h[c][:], pre[c][:], SILU, bias=bias[:, c : c + 1])
+        def edges(u):
+            return slice(u * HALF, (u + 1) * HALF)
 
-        update = [psum.tile([P, V], F32, name=f"update{e}") for e in range(OB)]
-        for c in range(HB):
+        pre = [[psum.tile([P, HALF], F32, name=f"pre{u}_{c}") for c in range(HB)] for u in range(2)]
+
+        def gathered_matmul(a, d, u, c):
+            first = (d * V + u * HALF) // GROUP
+            nc.tensor.matmul(
+                pre[u][c][:],
+                w1[d][:, a * H + c * P : a * H + (c + 1) * P],
+                nodes[a][:].indirect(offsets[:, first : first + HALF // GROUP]),
+                start=(a == 0 and d == 0),
+                stop=(a == KB - 1 and d == D - 1),
+            )
+
+        for d in range(D):
+            for u in range(2):
+                for c in range(HB):
+                    gathered_matmul(0, d, u, c)
+        for u in range(2):
+            for c in range(HB):
+                for d in range(D):
+                    gathered_matmul(1, d, u, c)
+
+        h = [[sbuf.tile([P, HALF], BF16, name=f"h{u}_{c}") for c in range(HB)] for u in range(2)]
+        for u in range(2):
+            for c in range(HB):
+                nc.scalar.activation(h[u][c][:], pre[u][c][:], SILU, bias=bias[:, c : c + 1])
+
+        for u in range(2):
+            update = [psum.tile([P, HALF], F32, name=f"update{u}_{e}") for e in range(OB)]
+            for c in range(HB):
+                for e in range(OB):
+                    nc.tensor.matmul(
+                        update[e][:], w2_t[:, c, e * P : (e + 1) * P], h[u][c][:],
+                        start=(c == 0), stop=(c == HB - 1),
+                    )
             for e in range(OB):
-                nc.tensor.matmul(
-                    update[e][:], w2_t[:, c, e * P : (e + 1) * P], h[c][:],
-                    start=(c == 0), stop=(c == HB - 1),
-                )
-        for e in range(OB):
-            result = sbuf.tile([P, V], F32, name=f"result{e}")
-            nc.vector.tensor_tensor(result[:], update[e][:], r_t[:, e, :], ADD)
-            nc.sync.dma_start(out[e * P : (e + 1) * P, :], result[:])
+                result = sbuf.tile([P, HALF], F32, name=f"result{u}_{e}")
+                nc.vector.tensor_tensor(result[:], update[e][:], r_t[:, e, edges(u)], ADD)
+                nc.sync.dma_start(out[e * P : (e + 1) * P, edges(u)], result[:])

@@ -6,6 +6,7 @@ P = 128
 GROUP = 16
 KB, HB, OB = K // P, H // P, O // P
 HALF = V // 2
+WARM_COLS = 304
 
 FLOPS = 2 * D * K * H * V + 2 * H * O * V
 
@@ -38,6 +39,11 @@ def tile_rows_edge2_silu_rep_kernel(tc, table, w, b, w2, r, offs, out):
         nc.sync.dma_start(nodes[1][:], table_blocks[1])
         nc.sync.dma_start(w2_t[:], w2.rearrange("(c p) o -> p c o", p=P))
         nc.sync.dma_start(r_t[:], r.rearrange("(e p) v -> p e v", p=P))
+
+        zeros = sbuf.tile([P, WARM_COLS], F32)
+        nc.vector.memset(zeros[:], 0.0)
+        unread = psum.tile([P, WARM_COLS], F32, tag="update1_1")
+        nc.tensor.matmul(unread[:], zeros[:, :P], zeros[:], start=True, stop=True)
 
         def edges(u):
             return slice(u * HALF, (u + 1) * HALF)

@@ -34,9 +34,9 @@ def tile_rows_edge2_silu_rep_kernel(tc, table, w, b, w2, r, offs, out):
         nc.sync.dma_start(nodes[0][:], table_blocks[0])
         nc.sync.dma_start(w1[0][:], w_ends[0])
         nc.sync.dma_start(offsets[:], offs)
-        nc.sync.dma_start(bias[:], b.rearrange("(c p) o -> p (c o)", p=P))
         nc.sync.dma_start(w1[1][:], w_ends[1])
         nc.sync.dma_start(nodes[1][:], table_blocks[1])
+        nc.sync.dma_start(bias[:], b.rearrange("(c p) o -> p (c o)", p=P))
         nc.sync.dma_start(w2_t[:], w2.rearrange("(c p) o -> p c o", p=P))
         nc.sync.dma_start(r_t[:], r.rearrange("(e p) v -> p e v", p=P))
 
@@ -44,6 +44,8 @@ def tile_rows_edge2_silu_rep_kernel(tc, table, w, b, w2, r, offs, out):
         nc.vector.memset(zeros[:], 0.0)
         unread = psum.tile([P, WARM_COLS], F32, tag="update1_1")
         nc.tensor.matmul(unread[:], zeros[:, :P], zeros[:], start=True, stop=True)
+        unread_silu = sbuf.tile([P, 1], F32)
+        nc.scalar.activation(unread_silu[:], zeros[:, :1], SILU)
 
         def edges(u):
             return slice(u * HALF, (u + 1) * HALF)

import concourse.mybir as mybir

S, K, V, D, H, O = 1024, 256, 256, 2, 256, 256
N = D * V
P = 128
GROUP = 16
KB, HB, OB = K // P, H // P, O // P
HALF = V // 2
WARM_COLS = 304

FLOPS = 2 * D * K * H * V + 2 * H * O * V

BF16, F32, U16 = mybir.dt.bfloat16, mybir.dt.float32, mybir.dt.uint16
SILU = mybir.ActivationFunctionType.Silu
ADD = mybir.AluOpType.add


def tile_rows_edge2_silu_rep_kernel(tc, table, w, b, w2, r, offs, out):
    nc = tc.nc
    with (
        tc.tile_pool(name="sbuf", bufs=1) as sbuf,
        tc.psum_pool(name="psum", bufs=1) as psum,
    ):
        table_blocks = table.rearrange("(p a) s -> a p s", a=KB)
        w_ends = w.rearrange("d (p a) i -> d p (a i)", a=KB)

        nodes = [sbuf.tile([P, S], BF16, name=f"nodes{a}") for a in range(KB)]
        w1 = [sbuf.tile([P, KB * H], BF16, name=f"w1_{d}") for d in range(D)]
        offsets = sbuf.tile([P, N // GROUP], U16)
        bias = sbuf.tile([P, HB], F32)
        w2_t = sbuf.tile([P, HB, O], BF16)
        r_t = sbuf.tile([P, OB, V], F32)

        nc.sync.dma_start(nodes[0][:], table_blocks[0])
        nc.sync.dma_start(w1[0][:], w_ends[0])
        nc.sync.dma_start(offsets[:], offs)
        nc.sync.dma_start(w1[1][:], w_ends[1])
        nc.sync.dma_start(nodes[1][:], table_blocks[1])
        nc.sync.dma_start(bias[:], b.rearrange("(c p) o -> p (c o)", p=P))
        nc.sync.dma_start(w2_t[:], w2.rearrange("(c p) o -> p c o", p=P))
        nc.sync.dma_start(r_t[:], r.rearrange("(e p) v -> p e v", p=P))

        zeros = sbuf.tile([P, WARM_COLS], F32)
        nc.vector.memset(zeros[:], 0.0)
        unread = psum.tile([P, WARM_COLS], F32, tag="update1_1")
        nc.tensor.matmul(unread[:], zeros[:, :P], zeros[:], start=True, stop=True)
        unread_silu = sbuf.tile([P, 1], F32)
        nc.scalar.activation(unread_silu[:], zeros[:, :1], SILU)

        def edges(u):
            return slice(u * HALF, (u + 1) * HALF)

        pre = [[psum.tile([P, HALF], F32, name=f"pre{u}_{c}") for c in range(HB)] for u in range(2)]

        def gathered_matmul(a, d, u, c):
            first = (d * V + u * HALF) // GROUP
            nc.tensor.matmul(
                pre[u][c][:],
                w1[d][:, a * H + c * P : a * H + (c + 1) * P],
                nodes[a][:].indirect(offsets[:, first : first + HALF // GROUP]),
                start=(a == 0 and d == 0),
                stop=(a == KB - 1 and d == D - 1),
            )

        for d in range(D):
            for u in range(2):
                for c in range(HB):
                    gathered_matmul(0, d, u, c)
        for u in range(2):
            for c in range(HB):
                for d in range(D):
                    gathered_matmul(1, d, u, c)

        h = [[sbuf.tile([P, HALF], BF16, name=f"h{u}_{c}") for c in range(HB)] for u in range(2)]
        for u in range(2):
            for c in range(HB):
                nc.scalar.activation(h[u][c][:], pre[u][c][:], SILU, bias=bias[:, c : c + 1])

        for u in range(2):
            update = [psum.tile([P, HALF], F32, name=f"update{u}_{e}") for e in range(OB)]
            for c in range(HB):
                for e in range(OB):
                    nc.tensor.matmul(
                        update[e][:], w2_t[:, c, e * P : (e + 1) * P], h[u][c][:],
                        start=(c == 0), stop=(c == HB - 1),
                    )
            for e in range(OB):
                result = sbuf.tile([P, HALF], F32, name=f"result{u}_{e}")
                nc.vector.tensor_tensor(result[:], update[e][:], r_t[:, e, edges(u)], ADD)
                nc.sync.dma_start(out[e * P : (e + 1) * P, edges(u)], result[:])
